import numpy as np
import ml_dtypes


def mxq(x, axis, fmt="e4m3"):
    dtype, down = {"e4m3": (ml_dtypes.float8_e4m3fn, 7), "e5m2": (ml_dtypes.float8_e5m2, 14)}[fmt]
    v = np.moveaxis(np.asarray(x, np.float32).astype(ml_dtypes.bfloat16).astype(np.float64), axis, -1)
    blocks = v.reshape(v.shape[:-1] + (-1, 32))
    amax = np.abs(blocks).max(-1, keepdims=True)
    byte = np.maximum(np.where(amax > 0, np.frexp(amax)[1] - 1 + 127, 0) - down, 1)
    scale = np.exp2(byte - 127.0)
    codes = (blocks / scale).astype(np.float32).astype(dtype).astype(np.float64)
    return np.moveaxis((codes * scale).reshape(v.shape), -1, axis)


WIDE = False


def mx_kscale(k):
    if not WIDE:
        return np.ones(k)
    levels = np.array([10, -10, 5, -5, 0])
    if k % 512:
        return np.exp2(np.random.permutation(np.resize(levels, k // 32))).repeat(32)
    a = np.empty((k // 512, 16))
    for p in range(k // 512):
        a[p, :8] = np.random.permutation(np.resize(levels, 8))
        for g in range(8):
            far = levels[np.abs(levels - a[p, g]) >= 10]
            a[p, g + 8] = far[np.random.randint(len(far))]
    return np.exp2(a.ravel()).repeat(32)


def f64(x):
    return np.asarray(x).astype(np.float64)


def striped(idx):
    return np.tile(idx.reshape(-1, 16).T, (8, 1)).astype(np.uint16)


def unstriped(offs):
    return offs[:16].T.reshape(-1).astype(np.int64)


def striped8(idx):
    return np.concatenate([x.reshape(-1, 16).T for x in idx]).astype(np.uint16)


def runs(offs, k):
    lists = np.stack([offs[16 * r : 16 * r + 16].T.reshape(-1) for r in range(8)]).astype(np.int64)
    return lists[np.arange(k) % 512 // 64]


def pack_weight(w):
    k, n = w.shape
    w = f64(np.asarray(w, np.float32).astype(ml_dtypes.bfloat16)).reshape(k // 32, 32, n)
    amax = np.abs(w).max(1)
    byte = np.clip(np.where(amax > 0, np.frexp(amax)[1] - 1 + 127 - 7, 1), 1, 254)
    scaled = (w * np.exp2(127.0 - byte)[:, None, :]).reshape(k, n).astype(np.float32)
    words = np.ascontiguousarray(scaled.reshape(k // 512, 128, 4, n).transpose(0, 1, 3, 2)).astype(ml_dtypes.float8_e4m3fn).view(np.uint8)
    return words, np.ascontiguousarray(byte.astype(np.uint8).reshape(k // 512, 16, n))


def unpack_weight(words, scales):
    g, p, n, _ = words.shape
    vals = np.ascontiguousarray(words).view(ml_dtypes.float8_e4m3fn).astype(np.float64) * np.repeat(np.exp2(scales.astype(np.float64) - 127.0), 8, axis=1)[..., None]
    return vals.transpose(0, 1, 3, 2).reshape(g * 512, n)


def sigmoid(v):
    return 1.0 / (1.0 + np.exp(-np.maximum(v, -700.0)))


K, T, S, H, C, U = 512, 2048, 256, 512, 512, 512


def setup_inputs():
    n = np.random.standard_normal
    s = mx_kscale(K)[:, None]
    packed_xT = pack_weight(n((K, T)) * s)
    packed_w1 = pack_weight(n((K, H)) / np.sqrt(2 * K) / s)
    packed_w2 = pack_weight(n((K, H)) / np.sqrt(2 * K) / s)
    perm = np.random.permutation(U)
    return {
        "x_words": packed_xT[0],
        "x_scales": packed_xT[1],
        "w1_words": packed_w1[0],
        "w1_scales": packed_w1[1],
        "w2_words": packed_w2[0],
        "w2_scales": packed_w2[1],
        "sl": np.random.uniform(1.0, 2.0, (H, 1)).astype(np.float32),
        "th": (0.5 * n((H, 1))).astype(np.float32),
        "gs": (np.random.uniform(0.5, 1.5, (K, 1)) / s).astype(np.float32),
        "offs": striped(np.random.permutation(T)[:S]),
        "hz": striped8(np.random.randint(0, T, (8, S))),
        "n1": striped(np.random.permutation(S)),
        "n2": striped(np.random.permutation(S)),
        "cand": striped(np.random.permutation(T)[:C]),
        "n3": striped(perm[:S]),
        "n4": striped(perm[S:]),
        "n5": striped(np.random.permutation(S)),
    }


def reference(x_words, x_scales, w1_words, w1_scales, w2_words, w2_scales, sl, th, gs, offs, hz, n1, n2, cand, n3, n4, n5):
    x_cand = unpack_weight(x_words, x_scales)[:, unstriped(cand)]
    xq = unpack_weight(x_words, x_scales)[:, unstriped(offs)]
    x_hz = unpack_weight(x_words, x_scales)[np.arange(K)[:, None], runs(hz, K)]
    y = unpack_weight(w1_words, w1_scales).T @ xq + unpack_weight(w2_words, w2_scales).T @ x_hz
    ds = np.zeros((H, S))
    ds[:, unstriped(n1)] = y
    sg = sigmoid(f64(sl) * (ds[:, unstriped(n2)] - f64(th)))
    z = f64(gs) * (y * sg)
    s = 0.0625 * ((x_cand.T @ mxq(z, 0, "e4m3")))
    dn = np.minimum(s, s[:, unstriped(n5)])
    up = np.maximum(s, s[:, unstriped(n5)])
    ph = np.zeros((C, U))
    ph[:, unstriped(n3)] = up
    out = ph.copy()
    out[:, unstriped(n4)] = dn
    return out

@@ -1,0 +1,217 @@
+from contextlib import ExitStack
+
+import concourse.mybir as mybir
+
+K, T, S, H, C, U = 512, 2048, 256, 512, 512, 512
+FLOPS = 2 * K * H * S * 2 + 2 * K * C * S
+
+F32 = mybir.dt.float32
+BF16 = mybir.dt.bfloat16
+I32 = mybir.dt.int32
+U32 = mybir.dt.uint32
+U16 = mybir.dt.uint16
+U8 = mybir.dt.uint8
+FP8X4 = mybir.dt.float8_e4m3fn_x4
+ALU = mybir.AluOpType
+ACT = mybir.ActivationFunctionType
+
+P = 128
+PACK = 4
+HALF = S // 2
+
+
+def tile_picked_thcerlpagmx_none_p_kernel(
+    tc, x_words, x_scales, w1_words, w1_scales, w2_words, w2_scales, sl, th, gs,
+    offs, hz, n1, n2, cand, n3, n4, n5, out,
+):
+    nc = tc.nc
+    with ExitStack() as ctx:
+        lists = ctx.enter_context(tc.tile_pool(name="lists", bufs=1))
+        keep = ctx.enter_context(tc.tile_pool(name="keep", bufs=1))
+        psum = ctx.enter_context(tc.psum_pool(name="psum", bufs=1))
+
+        def load_list(name, source):
+            tile = lists.tile(list(source.shape), U16, name=name)
+            nc.sync.dma_start(tile[:], source)
+            return tile
+
+        def words_of(dram):
+            return dram[0].rearrange("p n r -> p (n r)").bitcast(I32)
+
+        x_rows = keep.tile([P, T], U8, name="x_rows")
+        w_rows = keep.tile([P, 2 * H], U8, name="w_rows")
+        nc.gpsimd.memset(x_rows[:].bitcast(I32), 0)
+        nc.vector.memset(w_rows[:].bitcast(I32), 0)
+
+        hz_list = load_list("hz_list", hz)
+        offs_list = load_list("offs_list", offs)
+        for odd in range(2):
+            nc.sync.dma_start(x_rows[odd:P:16, :].bitcast(I32), x_scales[0][odd:16:2, :].bitcast(I32))
+        x_table = keep.tile([P, T], U32, name="x_table")
+        nc.sync.dma_start(x_table[:].bitcast(I32), words_of(x_words))
+        w_raw = []
+        for i, source in enumerate((w1_words, w2_words)):
+            raw = keep.tile([P, H], U32, name="w_raw%d" % i)
+            nc.sync.dma_start(raw[:].bitcast(I32), words_of(source))
+            w_raw.append(raw)
+
+        for i, source in enumerate((w1_scales, w2_scales)):
+            nc.scalar.dma_start(w_rows[0:P:8, i * H:(i + 1) * H].bitcast(I32), source[0].bitcast(I32))
+
+        per_row = []
+        for name, source in (("slope", sl), ("threshold", th), ("gain", gs)):
+            tile = keep.tile([P, PACK], F32, name=name)
+            nc.gpsimd.dma_start(tile[:], source.rearrange("(p t) o -> p (t o)", t=PACK))
+            per_row.append(tile)
+        slope, threshold, gain = per_row
+
+        def scale_plane(picked_bytes, name, tag, queue):
+            plane = keep.tile([P, 2 * S], U8, name=name, tag=tag, align_bytes=64)
+            nc.vector.tensor_copy(plane[:].bitcast(I32), picked_bytes[:].bitcast(I32))
+            for r in range(2):
+                queue.dma_start(plane[2 + r:P:32, :].bitcast(I32), picked_bytes[16 + r:P:32, :].bitcast(I32))
+            return plane
+
+        for r in range(1, 4):
+            nc.sync.dma_start(w_rows[r:P:32, :].bitcast(I32), w_rows[8 * r:P:32, :].bitcast(I32))
+
+        pair_bytes = keep.tile([P, 2 * S], U8, name="pair_bytes", align_bytes=64)
+        nc.vector.tensor_copy(pair_bytes[:, S:], x_rows[:].indirect(hz_list[:]))
+        nc.vector.tensor_copy(pair_bytes[:, :S], x_rows[:].indirect(offs_list[:]))
+        pair_plane = scale_plane(pair_bytes, "pair_plane", "bytes_a", nc.sync)
+
+        n1_list = load_list("n1_list", n1)
+        n2_list = load_list("n2_list", n2)
+        cand_list = load_list("cand_list", cand)
+        n5_list = load_list("n5_list", n5)
+        n3_list = load_list("n3_list", n3)
+        n4_list = load_list("n4_list", n4)
+
+        pair_words = keep.tile([P, 2 * S], U32, name="pair_words", tag="picked_words", align_bytes=64)
+        nc.vector.tensor_copy(pair_words[:, :S], x_table[:].indirect(offs_list[:]))
+        nc.vector.tensor_copy(pair_words[:, S:], x_table[:].indirect(hz_list[:]))
+
+        w1_dealt = keep.tile([P, PACK, P], U32, name="w1_dealt", align_bytes=64)
+        nc.scalar.copy(w1_dealt[:].rearrange("p t m -> p m t"), w_raw[0][:].rearrange("p (m t) -> p m t", t=PACK))
+        w2_first = keep.tile([P, P], U32, name="w2_first", align_bytes=64)
+        w2_rest = keep.tile([P, PACK - 1, P], U32, name="w2_rest", align_bytes=64)
+        w2_view = w_raw[1][:].rearrange("p (m t) -> p m t", t=PACK)
+        nc.scalar.copy(w2_first[:], w2_view[:, :, 0])
+        nc.scalar.copy(w2_rest[:].rearrange("p t m -> p m t"), w2_view[:, :, 1:PACK])
+        w2_dealt = [w2_first[:]] + [w2_rest[:, t, :] for t in range(PACK - 1)]
+
+        bias = keep.tile([P, PACK], F32, name="bias")
+        product = keep.tile([P, PACK], F32, name="product")
+        nc.gpsimd.tensor_tensor(product[:], slope[:], threshold[:], ALU.mult)
+        nc.gpsimd.tensor_scalar(bias[:], product[:], -1.0, 0.0, ALU.mult, ALU.add)
+
+        y_banks, y_tiles = [], []
+        for t in range(PACK):
+            w_plane = keep.tile([P, 2 * P], U8, name="w_plane%d" % t, align_bytes=64)
+            nc.vector.tensor_copy(w_plane[:], w_rows[:].rearrange("p (m t) -> p m t", t=PACK)[:, :, t])
+            bank = psum.tile([P, S], F32, name="y_bank%d" % t)
+            for i, codes in enumerate((w1_dealt[:, t, :], w2_dealt[t])):
+                nc.tensor.matmul_mx(
+                    out=bank[:],
+                    lhsT=codes.bitcast(FP8X4),
+                    lhsT_scale=w_plane[:, i * P:(i + 1) * P],
+                    rhs=pair_words[:, i * S:(i + 1) * S].bitcast(FP8X4),
+                    rhs_scale=pair_plane[:, i * S:(i + 1) * S],
+                    start=(i == 0),
+                    stop=(i == 1),
+                )
+            y = keep.tile([P, S], F32, name="y%d" % t)
+            nc.vector.tensor_copy(y[:], bank[:])
+            y_banks.append(bank)
+            y_tiles.append(y)
+
+        cand_bytes = keep.tile([P, C], U8, name="cand_bytes", tag="bytes_a", align_bytes=64)
+        nc.vector.tensor_copy(cand_bytes[:], x_rows[:].indirect(cand_list[:]))
+        cand_plane = scale_plane(cand_bytes, "cand_plane", "bytes_b", nc.sync)
+        cand_words = keep.tile([P, C], U32, name="cand_words", tag="picked_words", align_bytes=64)
+        nc.vector.tensor_copy(cand_words[:], x_table[:].indirect(cand_list[:]))
+
+        z_halves = [keep.tile([P, HALF, PACK], BF16, name="z%d" % h, align_bytes=64) for h in range(2)]
+        ds_tiles = [keep.tile([P, 2 * S], F32, name="ds%d" % t) for t in range(PACK)]
+
+        def place_y(t):
+            nc.scalar.activation(ds_tiles[t][:].indirect(n1_list[:]), y_tiles[t][:], ACT.Copy)
+
+        def gate(t, pieces):
+            width = S // pieces
+            sg = keep.tile([P, S], F32, name="sg%d" % t)
+            for piece in range(pieces):
+                nc.scalar.activation(
+                    sg[:, piece * width:(piece + 1) * width],
+                    ds_tiles[t][:].indirect(n2_list[:, piece * width // 16:(piece + 1) * width // 16]),
+                    ACT.Sigmoid, bias=bias[:, t:t + 1], scale=slope[:, t:t + 1],
+                )
+            for h in range(2):
+                cols = slice(h * HALF, (h + 1) * HALF)
+                nc.vector.scalar_tensor_tensor(
+                    z_halves[h][:, :, t], y_banks[t][:, cols], gain[:, t:t + 1], sg[:, cols], ALU.mult, ALU.mult
+                )
+
+        place_y(0)
+        place_y(1)
+        gate(0, 1)
+        place_y(2)
+        gate(1, 1)
+        gate(2, 1)
+        place_y(3)
+        gate(3, 2)
+
+        z_codes = keep.tile([P, S], U32, name="z_codes", align_bytes=64)
+        z_plane = keep.tile([P, S], U8, name="z_plane", align_bytes=64)
+        for h in range(2):
+            cols = slice(h * HALF, (h + 1) * HALF)
+            nc.vector.quantize_mx(
+                out=z_codes[:, cols].bitcast(FP8X4), scales=z_plane[:, cols],
+                in_=z_halves[h][:].rearrange("p j t -> p (j t)"),
+            )
+
+        s_tiles, pages, ups, downs = [], [], [], []
+
+        def score(c):
+            rows = slice(c * P, (c + 1) * P)
+            s = keep.tile([P, 2 * S], F32, name="s%d" % c)
+            for h in range(2):
+                cols = slice(h * HALF, (h + 1) * HALF)
+                bank = psum.tile([P, HALF], F32, name="s_bank%d_%d" % (c, h), tag="s_bank%d" % ((2 * c + h) % 4))
+                nc.tensor.matmul_mx(
+                    out=bank[:],
+                    lhsT=cand_words[:, rows].bitcast(FP8X4), lhsT_scale=cand_plane[:, rows],
+                    rhs=z_codes[:, cols].bitcast(FP8X4), rhs_scale=z_plane[:, cols],
+                    start=True, stop=True,
+                )
+                nc.vector.tensor_scalar(s[:, cols], bank[:], 0.0625, None, ALU.mult)
+            s_tiles.append(s)
+
+        def partner(c):
+            other = keep.tile([P, S], F32, name="other%d" % c)
+            nc.scalar.activation(other[:], s_tiles[c][:].indirect(n5_list[:]), ACT.Copy)
+            up = keep.tile([P, S], F32, name="up%d" % c)
+            down = keep.tile([P, S], F32, name="down%d" % c)
+            nc.vector.tensor_tensor(up[:], s_tiles[c][:, :S], other[:], ALU.max)
+            nc.vector.tensor_tensor(down[:], s_tiles[c][:, :S], other[:], ALU.min)
+            ups.append(up)
+            downs.append(down)
+
+        def place_up(c):
+            page = keep.tile([P, U], F32, name="page%d" % c)
+            nc.scalar.activation(page[:].indirect(n3_list[:]), ups[c][:], ACT.Copy)
+            pages.append(page)
+
+        def place_down(c):
+            nc.scalar.activation(pages[c][:].indirect(n4_list[:]), downs[c][:], ACT.Copy)
+            nc.sync.dma_start(out[c * P:(c + 1) * P, :], pages[c][:])
+
+        for c in range(4):
+            score(c)
+        for c in (0, 2):
+            partner(c)
+            partner(c + 1)
+            place_up(c)
+            place_up(c + 1)
+            place_down(c)
+            place_down(c + 1)

@@ -58,6 +58,11 @@ def tile_picked_thcerlpagmx_none_p_kernel(
         for i, source in enumerate((w1_scales, w2_scales)):
             nc.scalar.dma_start(w_rows[0:P:8, i * H:(i + 1) * H].bitcast(I32), source[0].bitcast(I32))
 
+        warm_in = keep.tile([P, 1], F32, name="warm_in")
+        warm_out = keep.tile([P, 1], F32, name="warm_out")
+        nc.vector.memset(warm_in[:], 0.0)
+        nc.scalar.activation(warm_out[:], warm_in[:], ACT.Sigmoid)
+
         per_row = []
         for name, source in (("slope", sl), ("threshold", th), ("gain", gs)):
             tile = keep.tile([P, PACK], F32, name=name)

@@ -45,6 +45,7 @@ def tile_picked_thcerlpagmx_none_p_kernel(
 
         hz_list = load_list("hz_list", hz)
         offs_list = load_list("offs_list", offs)
+        n1_list = load_list("n1_list", n1)
         for odd in range(2):
             nc.sync.dma_start(x_rows[odd:P:16, :].bitcast(I32), x_scales[0][odd:16:2, :].bitcast(I32))
         x_table = keep.tile([P, T], U32, name="x_table")
@@ -85,7 +86,6 @@ def tile_picked_thcerlpagmx_none_p_kernel(
         nc.vector.tensor_copy(pair_bytes[:, :S], x_rows[:].indirect(offs_list[:]))
         pair_plane = scale_plane(pair_bytes, "pair_plane", "bytes_a", nc.sync)
 
-        n1_list = load_list("n1_list", n1)
         n2_list = load_list("n2_list", n2)
         cand_list = load_list("cand_list", cand)
         n5_list = load_list("n5_list", n5)
@@ -112,7 +112,7 @@ def tile_picked_thcerlpagmx_none_p_kernel(
 
         y_banks, y_tiles = [], []
         for t in range(PACK):
-            w_plane = keep.tile([P, 2 * P], U8, name="w_plane%d" % t, align_bytes=64)
+            w_plane = keep.tile([P, 2 * P], U8, name="w_plane%d" % t, tag="w_plane", bufs=2, align_bytes=64)
             nc.vector.tensor_copy(w_plane[:], w_rows[:].rearrange("p (m t) -> p m t", t=PACK)[:, :, t])
             bank = psum.tile([P, S], F32, name="y_bank%d" % t)
             for i, codes in enumerate((w1_dealt[:, t, :], w2_dealt[t])):
@@ -144,7 +144,10 @@ def tile_picked_thcerlpagmx_none_p_kernel(
 
         def gate(t, pieces):
             width = S // pieces
-            sg = keep.tile([P, S], F32, name="sg%d" % t)
+            if t < 2:
+                sg = keep.tile([P, S], F32, name="sg%d" % t, tag="w_plane", bufs=2, align_bytes=64)
+            else:
+                sg = keep.tile([P, S], F32, name="sg%d" % t)
             for piece in range(pieces):
                 nc.scalar.activation(
                     sg[:, piece * width:(piece + 1) * width],
@@ -175,48 +178,57 @@ def tile_picked_thcerlpagmx_none_p_kernel(
                 in_=z_halves[h][:].rearrange("p j t -> p (j t)"),
             )
 
-        s_tiles, pages, ups, downs = [], [], [], []
+        s_tiles, others, pages = [], [], []
 
         def score(c):
             rows = slice(c * P, (c + 1) * P)
             s = keep.tile([P, 2 * S], F32, name="s%d" % c)
-            for h in range(2):
-                cols = slice(h * HALF, (h + 1) * HALF)
-                bank = psum.tile([P, HALF], F32, name="s_bank%d_%d" % (c, h), tag="s_bank%d" % ((2 * c + h) % 4))
+            pieces = 2 if c == 0 else 1
+            width = S // pieces
+            for piece in range(pieces):
+                cols = slice(piece * width, (piece + 1) * width)
+                bank = psum.tile([P, width], F32, name="s_bank%d_%d" % (c, piece),
+                                 tag="y_bank0" if c == 3 else "s_bank%d_%d" % (c, piece))
                 nc.tensor.matmul_mx(
                     out=bank[:],
                     lhsT=cand_words[:, rows].bitcast(FP8X4), lhsT_scale=cand_plane[:, rows],
                     rhs=z_codes[:, cols].bitcast(FP8X4), rhs_scale=z_plane[:, cols],
                     start=True, stop=True,
                 )
-                nc.vector.tensor_scalar(s[:, cols], bank[:], 0.0625, None, ALU.mult)
+                if c == 0:
+                    nc.scalar.activation(s[:, cols], bank[:], ACT.Copy, scale=0.0625)
+                else:
+                    nc.vector.tensor_scalar(s[:, cols], bank[:], 0.0625, None, ALU.mult)
             s_tiles.append(s)
 
         def partner(c):
             other = keep.tile([P, S], F32, name="other%d" % c)
             nc.scalar.activation(other[:], s_tiles[c][:].indirect(n5_list[:]), ACT.Copy)
-            up = keep.tile([P, S], F32, name="up%d" % c)
-            down = keep.tile([P, S], F32, name="down%d" % c)
-            nc.vector.tensor_tensor(up[:], s_tiles[c][:, :S], other[:], ALU.max)
-            nc.vector.tensor_tensor(down[:], s_tiles[c][:, :S], other[:], ALU.min)
-            ups.append(up)
-            downs.append(down)
+            others.append(other)
 
-        def place_up(c):
+        def pick(c, op, name):
+            picked = keep.tile([P, S], F32, name="%s%d" % (name, c))
+            nc.vector.tensor_tensor(picked[:], s_tiles[c][:, :S], others[c][:], op)
+            return picked
+
+        def place_up(c, up):
             page = keep.tile([P, U], F32, name="page%d" % c)
-            nc.scalar.activation(page[:].indirect(n3_list[:]), ups[c][:], ACT.Copy)
+            nc.scalar.activation(page[:].indirect(n3_list[:]), up[:], ACT.Copy)
             pages.append(page)
 
-        def place_down(c):
-            nc.scalar.activation(pages[c][:].indirect(n4_list[:]), downs[c][:], ACT.Copy)
+        def place_down(c, down):
+            nc.scalar.activation(pages[c][:].indirect(n4_list[:]), down[:], ACT.Copy)
             nc.sync.dma_start(out[c * P:(c + 1) * P, :], pages[c][:])
 
-        for c in range(4):
-            score(c)
-        for c in (0, 2):
-            partner(c)
-            partner(c + 1)
-            place_up(c)
-            place_up(c + 1)
-            place_down(c)
-            place_down(c + 1)
+        for first in (0, 2):
+            pair = (first, first + 1)
+            for c in pair:
+                score(c)
+            for c in pair:
+                partner(c)
+            ups = [pick(c, ALU.max, "up") for c in pair]
+            downs = [pick(c, ALU.min, "down") for c in pair]
+            for c, up in zip(pair, ups):
+                place_up(c, up)
+            for c, down in zip(pair, downs):
+                place_down(c, down)

@@ -17,7 +17,14 @@ ACT = mybir.ActivationFunctionType
 
 P = 128
 PACK = 4
+QUADRANT = 32
+GROUP = 16
+BLOCK = 8
+SCALE_ROWS = K // 32
+CAND_TILES = C // P
 HALF = S // 2
+WINDOW = 2 * S
+MX_ALIGN = 64
 
 
 def tile_picked_thcerlpagmx_none_p_kernel(
@@ -47,7 +54,7 @@ def tile_picked_thcerlpagmx_none_p_kernel(
         offs_list = load_list("offs_list", offs)
         n1_list = load_list("n1_list", n1)
         for odd in range(2):
-            nc.sync.dma_start(x_rows[odd:P:16, :].bitcast(I32), x_scales[0][odd:16:2, :].bitcast(I32))
+            nc.sync.dma_start(x_rows[odd:P:GROUP, :].bitcast(I32), x_scales[0][odd:SCALE_ROWS:2, :].bitcast(I32))
         x_table = keep.tile([P, T], U32, name="x_table")
         nc.sync.dma_start(x_table[:].bitcast(I32), words_of(x_words))
         w_raw = []
@@ -57,7 +64,7 @@ def tile_picked_thcerlpagmx_none_p_kernel(
             w_raw.append(raw)
 
         for i, source in enumerate((w1_scales, w2_scales)):
-            nc.scalar.dma_start(w_rows[0:P:8, i * H:(i + 1) * H].bitcast(I32), source[0].bitcast(I32))
+            nc.scalar.dma_start(w_rows[0:P:BLOCK, i * H:(i + 1) * H].bitcast(I32), source[0].bitcast(I32))
 
         warm_in = keep.tile([P, 1], F32, name="warm_in")
         warm_out = keep.tile([P, 1], F32, name="warm_out")
@@ -71,20 +78,22 @@ def tile_picked_thcerlpagmx_none_p_kernel(
             per_row.append(tile)
         slope, threshold, gain = per_row
 
-        def scale_plane(picked_bytes, name, tag, queue):
-            plane = keep.tile([P, 2 * S], U8, name=name, tag=tag, align_bytes=64)
+        for r in range(1, PACK):
+            nc.sync.dma_start(w_rows[r:P:QUADRANT, :].bitcast(I32), w_rows[BLOCK * r:P:QUADRANT, :].bitcast(I32))
+
+        def scale_plane(picked_bytes, name, tag):
+            plane = keep.tile([P, picked_bytes[:].shape[1]], U8, name=name, tag=tag, align_bytes=MX_ALIGN)
             nc.vector.tensor_copy(plane[:].bitcast(I32), picked_bytes[:].bitcast(I32))
             for r in range(2):
-                queue.dma_start(plane[2 + r:P:32, :].bitcast(I32), picked_bytes[16 + r:P:32, :].bitcast(I32))
+                nc.sync.dma_start(
+                    plane[2 + r:P:QUADRANT, :].bitcast(I32), picked_bytes[GROUP + r:P:QUADRANT, :].bitcast(I32)
+                )
             return plane
 
-        for r in range(1, 4):
-            nc.sync.dma_start(w_rows[r:P:32, :].bitcast(I32), w_rows[8 * r:P:32, :].bitcast(I32))
-
-        pair_bytes = keep.tile([P, 2 * S], U8, name="pair_bytes", align_bytes=64)
+        pair_bytes = keep.tile([P, 2 * S], U8, name="pair_bytes", align_bytes=MX_ALIGN)
         nc.vector.tensor_copy(pair_bytes[:, S:], x_rows[:].indirect(hz_list[:]))
         nc.vector.tensor_copy(pair_bytes[:, :S], x_rows[:].indirect(offs_list[:]))
-        pair_plane = scale_plane(pair_bytes, "pair_plane", "bytes_a", nc.sync)
+        pair_plane = scale_plane(pair_bytes, "pair_plane", "pair_plane_then_cand_bytes")
 
         n2_list = load_list("n2_list", n2)
         cand_list = load_list("cand_list", cand)
@@ -92,14 +101,14 @@ def tile_picked_thcerlpagmx_none_p_kernel(
         n3_list = load_list("n3_list", n3)
         n4_list = load_list("n4_list", n4)
 
-        pair_words = keep.tile([P, 2 * S], U32, name="pair_words", tag="picked_words", align_bytes=64)
+        pair_words = keep.tile([P, 2 * S], U32, name="pair_words", tag="picked_words", align_bytes=MX_ALIGN)
         nc.vector.tensor_copy(pair_words[:, :S], x_table[:].indirect(offs_list[:]))
         nc.vector.tensor_copy(pair_words[:, S:], x_table[:].indirect(hz_list[:]))
 
-        w1_dealt = keep.tile([P, PACK, P], U32, name="w1_dealt", align_bytes=64)
+        w1_dealt = keep.tile([P, PACK, P], U32, name="w1_dealt", align_bytes=MX_ALIGN)
         nc.scalar.copy(w1_dealt[:].rearrange("p t m -> p m t"), w_raw[0][:].rearrange("p (m t) -> p m t", t=PACK))
-        w2_first = keep.tile([P, P], U32, name="w2_first", align_bytes=64)
-        w2_rest = keep.tile([P, PACK - 1, P], U32, name="w2_rest", align_bytes=64)
+        w2_first = keep.tile([P, P], U32, name="w2_first", align_bytes=MX_ALIGN)
+        w2_rest = keep.tile([P, PACK - 1, P], U32, name="w2_rest", align_bytes=MX_ALIGN)
         w2_view = w_raw[1][:].rearrange("p (m t) -> p m t", t=PACK)
         nc.scalar.copy(w2_first[:], w2_view[:, :, 0])
         nc.scalar.copy(w2_rest[:].rearrange("p t m -> p m t"), w2_view[:, :, 1:PACK])
@@ -112,7 +121,7 @@ def tile_picked_thcerlpagmx_none_p_kernel(
 
         y_banks, y_tiles = [], []
         for t in range(PACK):
-            w_plane = keep.tile([P, 2 * P], U8, name="w_plane%d" % t, tag="w_plane", bufs=2, align_bytes=64)
+            w_plane = keep.tile([P, 2 * P], U8, name="w_plane%d" % t, tag="w_plane", bufs=2, align_bytes=MX_ALIGN)
             nc.vector.tensor_copy(w_plane[:], w_rows[:].rearrange("p (m t) -> p m t", t=PACK)[:, :, t])
             bank = psum.tile([P, S], F32, name="y_bank%d" % t)
             for i, codes in enumerate((w1_dealt[:, t, :], w2_dealt[t])):
@@ -130,31 +139,32 @@ def tile_picked_thcerlpagmx_none_p_kernel(
             y_banks.append(bank)
             y_tiles.append(y)
 
-        cand_bytes = keep.tile([P, C], U8, name="cand_bytes", tag="bytes_a", align_bytes=64)
+        cand_bytes = keep.tile([P, C], U8, name="cand_bytes", tag="pair_plane_then_cand_bytes", align_bytes=MX_ALIGN)
         nc.vector.tensor_copy(cand_bytes[:], x_rows[:].indirect(cand_list[:]))
-        cand_plane = scale_plane(cand_bytes, "cand_plane", "bytes_b", nc.sync)
-        cand_words = keep.tile([P, C], U32, name="cand_words", tag="picked_words", align_bytes=64)
+        cand_plane = scale_plane(cand_bytes, "cand_plane", "cand_plane")
+        cand_words = keep.tile([P, C], U32, name="cand_words", tag="picked_words", align_bytes=MX_ALIGN)
         nc.vector.tensor_copy(cand_words[:], x_table[:].indirect(cand_list[:]))
 
-        z_halves = [keep.tile([P, HALF, PACK], BF16, name="z%d" % h, align_bytes=64) for h in range(2)]
-        ds_tiles = [keep.tile([P, 2 * S], F32, name="ds%d" % t) for t in range(PACK)]
+        z_halves = [keep.tile([P, HALF, PACK], BF16, name="z%d" % h, align_bytes=MX_ALIGN) for h in range(2)]
+        ds_tiles = [keep.tile([P, WINDOW], F32, name="ds%d" % t) for t in range(PACK)]
+        sg_tiles = []
 
         def place_y(t):
             nc.scalar.activation(ds_tiles[t][:].indirect(n1_list[:]), y_tiles[t][:], ACT.Copy)
 
-        def gate(t, pieces):
-            width = S // pieces
-            if t < 2:
-                sg = keep.tile([P, S], F32, name="sg%d" % t, tag="w_plane", bufs=2, align_bytes=64)
-            else:
-                sg = keep.tile([P, S], F32, name="sg%d" % t)
-            for piece in range(pieces):
-                nc.scalar.activation(
-                    sg[:, piece * width:(piece + 1) * width],
-                    ds_tiles[t][:].indirect(n2_list[:, piece * width // 16:(piece + 1) * width // 16]),
-                    ACT.Sigmoid, bias=bias[:, t:t + 1], scale=slope[:, t:t + 1],
-                )
-            for h in range(2):
+        def gate(t, first, last):
+            if first == 0:
+                if t < 2:
+                    sg_tiles.append(keep.tile([P, S], F32, name="sg%d" % t, tag="w_plane", bufs=2, align_bytes=MX_ALIGN))
+                else:
+                    sg_tiles.append(keep.tile([P, S], F32, name="sg%d" % t))
+            sg = sg_tiles[t]
+            nc.scalar.activation(
+                sg[:, first * HALF:last * HALF],
+                ds_tiles[t][:].indirect(n2_list[:, first * HALF // GROUP:last * HALF // GROUP]),
+                ACT.Sigmoid, bias=bias[:, t:t + 1], scale=slope[:, t:t + 1],
+            )
+            for h in range(first, last):
                 cols = slice(h * HALF, (h + 1) * HALF)
                 nc.vector.scalar_tensor_tensor(
                     z_halves[h][:, :, t], y_banks[t][:, cols], gain[:, t:t + 1], sg[:, cols], ALU.mult, ALU.mult
@@ -162,15 +172,17 @@ def tile_picked_thcerlpagmx_none_p_kernel(
 
         place_y(0)
         place_y(1)
-        gate(0, 1)
+        gate(0, 0, 2)
         place_y(2)
-        gate(1, 1)
-        gate(2, 1)
+        gate(1, 0, 2)
+        gate(2, 0, 1)
         place_y(3)
-        gate(3, 2)
+        gate(2, 1, 2)
+        gate(3, 0, 1)
+        gate(3, 1, 2)
 
-        z_codes = keep.tile([P, S], U32, name="z_codes", align_bytes=64)
-        z_plane = keep.tile([P, S], U8, name="z_plane", align_bytes=64)
+        z_codes = keep.tile([P, S], U32, name="z_codes", align_bytes=MX_ALIGN)
+        z_plane = keep.tile([P, S], U8, name="z_plane", align_bytes=MX_ALIGN)
         for h in range(2):
             cols = slice(h * HALF, (h + 1) * HALF)
             nc.vector.quantize_mx(
@@ -182,13 +194,13 @@ def tile_picked_thcerlpagmx_none_p_kernel(
 
         def score(c):
             rows = slice(c * P, (c + 1) * P)
-            s = keep.tile([P, 2 * S], F32, name="s%d" % c)
+            s = keep.tile([P, WINDOW], F32, name="s%d" % c)
             pieces = 2 if c == 0 else 1
             width = S // pieces
             for piece in range(pieces):
                 cols = slice(piece * width, (piece + 1) * width)
                 bank = psum.tile([P, width], F32, name="s_bank%d_%d" % (c, piece),
-                                 tag="y_bank0" if c == 3 else "s_bank%d_%d" % (c, piece))
+                                 tag="y_bank0" if c == CAND_TILES - 1 else "s_bank%d_%d" % (c, piece))
                 nc.tensor.matmul_mx(
                     out=bank[:],
                     lhsT=cand_words[:, rows].bitcast(FP8X4), lhsT_scale=cand_plane[:, rows],
@@ -220,12 +232,12 @@ def tile_picked_thcerlpagmx_none_p_kernel(
             nc.scalar.activation(pages[c][:].indirect(n4_list[:]), down[:], ACT.Copy)
             nc.sync.dma_start(out[c * P:(c + 1) * P, :], pages[c][:])
 
-        for first in (0, 2):
+        for c in range(CAND_TILES):
+            score(c)
+        for c in range(CAND_TILES):
+            partner(c)
+        for first in range(0, CAND_TILES, 2):
             pair = (first, first + 1)
-            for c in pair:
-                score(c)
-            for c in pair:
-                partner(c)
             ups = [pick(c, ALU.max, "up") for c in pair]
             downs = [pick(c, ALU.min, "down") for c in pair]
             for c, up in zip(pair, ups):

from contextlib import ExitStack

import concourse.mybir as mybir

K, T, S, H, C, U = 512, 2048, 256, 512, 512, 512
FLOPS = 2 * K * H * S * 2 + 2 * K * C * S

F32 = mybir.dt.float32
BF16 = mybir.dt.bfloat16
I32 = mybir.dt.int32
U32 = mybir.dt.uint32
U16 = mybir.dt.uint16
U8 = mybir.dt.uint8
FP8X4 = mybir.dt.float8_e4m3fn_x4
ALU = mybir.AluOpType
ACT = mybir.ActivationFunctionType

P = 128
PACK = 4
QUADRANT = 32
GROUP = 16
BLOCK = 8
SCALE_ROWS = K // 32
CAND_TILES = C // P
HALF = S // 2
WINDOW = 2 * S
MX_ALIGN = 64


def tile_picked_thcerlpagmx_none_p_kernel(
    tc, x_words, x_scales, w1_words, w1_scales, w2_words, w2_scales, sl, th, gs,
    offs, hz, n1, n2, cand, n3, n4, n5, out,
):
    nc = tc.nc
    with ExitStack() as ctx:
        lists = ctx.enter_context(tc.tile_pool(name="lists", bufs=1))
        keep = ctx.enter_context(tc.tile_pool(name="keep", bufs=1))
        psum = ctx.enter_context(tc.psum_pool(name="psum", bufs=1))

        def load_list(name, source):
            tile = lists.tile(list(source.shape), U16, name=name)
            nc.sync.dma_start(tile[:], source)
            return tile

        def words_of(dram):
            return dram[0].rearrange("p n r -> p (n r)").bitcast(I32)

        x_rows = keep.tile([P, T], U8, name="x_rows")
        w_rows = keep.tile([P, 2 * H], U8, name="w_rows")
        nc.gpsimd.memset(x_rows[:].bitcast(I32), 0)
        nc.vector.memset(w_rows[:].bitcast(I32), 0)

        hz_list = load_list("hz_list", hz)
        offs_list = load_list("offs_list", offs)
        n1_list = load_list("n1_list", n1)
        for odd in range(2):
            nc.sync.dma_start(x_rows[odd:P:GROUP, :].bitcast(I32), x_scales[0][odd:SCALE_ROWS:2, :].bitcast(I32))
        x_table = keep.tile([P, T], U32, name="x_table")
        nc.sync.dma_start(x_table[:].bitcast(I32), words_of(x_words))
        w_raw = []
        for i, source in enumerate((w1_words, w2_words)):
            raw = keep.tile([P, H], U32, name="w_raw%d" % i)
            nc.sync.dma_start(raw[:].bitcast(I32), words_of(source))
            w_raw.append(raw)

        for i, source in enumerate((w1_scales, w2_scales)):
            nc.scalar.dma_start(w_rows[0:P:BLOCK, i * H:(i + 1) * H].bitcast(I32), source[0].bitcast(I32))

        warm_in = keep.tile([P, 1], F32, name="warm_in")
        warm_out = keep.tile([P, 1], F32, name="warm_out")
        nc.vector.memset(warm_in[:], 0.0)
        nc.scalar.activation(warm_out[:], warm_in[:], ACT.Sigmoid)

        per_row = []
        for name, source in (("slope", sl), ("threshold", th), ("gain", gs)):
            tile = keep.tile([P, PACK], F32, name=name)
            nc.gpsimd.dma_start(tile[:], source.rearrange("(p t) o -> p (t o)", t=PACK))
            per_row.append(tile)
        slope, threshold, gain = per_row

        for r in range(1, PACK):
            nc.sync.dma_start(w_rows[r:P:QUADRANT, :].bitcast(I32), w_rows[BLOCK * r:P:QUADRANT, :].bitcast(I32))

        def scale_plane(picked_bytes, name, tag):
            plane = keep.tile([P, picked_bytes[:].shape[1]], U8, name=name, tag=tag, align_bytes=MX_ALIGN)
            nc.vector.tensor_copy(plane[:].bitcast(I32), picked_bytes[:].bitcast(I32))
            for r in range(2):
                nc.sync.dma_start(
                    plane[2 + r:P:QUADRANT, :].bitcast(I32), picked_bytes[GROUP + r:P:QUADRANT, :].bitcast(I32)
                )
            return plane

        pair_bytes = keep.tile([P, 2 * S], U8, name="pair_bytes", align_bytes=MX_ALIGN)
        nc.vector.tensor_copy(pair_bytes[:, S:], x_rows[:].indirect(hz_list[:]))
        nc.vector.tensor_copy(pair_bytes[:, :S], x_rows[:].indirect(offs_list[:]))
        pair_plane = scale_plane(pair_bytes, "pair_plane", "pair_plane_then_cand_bytes")

        n2_list = load_list("n2_list", n2)
        cand_list = load_list("cand_list", cand)
        n5_list = load_list("n5_list", n5)
        n3_list = load_list("n3_list", n3)
        n4_list = load_list("n4_list", n4)

        pair_words = keep.tile([P, 2 * S], U32, name="pair_words", tag="picked_words", align_bytes=MX_ALIGN)
        nc.vector.tensor_copy(pair_words[:, :S], x_table[:].indirect(offs_list[:]))
        nc.vector.tensor_copy(pair_words[:, S:], x_table[:].indirect(hz_list[:]))

        w1_dealt = keep.tile([P, PACK, P], U32, name="w1_dealt", align_bytes=MX_ALIGN)
        nc.scalar.copy(w1_dealt[:].rearrange("p t m -> p m t"), w_raw[0][:].rearrange("p (m t) -> p m t", t=PACK))
        w2_first = keep.tile([P, P], U32, name="w2_first", align_bytes=MX_ALIGN)
        w2_rest = keep.tile([P, PACK - 1, P], U32, name="w2_rest", align_bytes=MX_ALIGN)
        w2_view = w_raw[1][:].rearrange("p (m t) -> p m t", t=PACK)
        nc.scalar.copy(w2_first[:], w2_view[:, :, 0])
        nc.scalar.copy(w2_rest[:].rearrange("p t m -> p m t"), w2_view[:, :, 1:PACK])
        w2_dealt = [w2_first[:]] + [w2_rest[:, t, :] for t in range(PACK - 1)]

        bias = keep.tile([P, PACK], F32, name="bias")
        product = keep.tile([P, PACK], F32, name="product")
        nc.gpsimd.tensor_tensor(product[:], slope[:], threshold[:], ALU.mult)
        nc.gpsimd.tensor_scalar(bias[:], product[:], -1.0, 0.0, ALU.mult, ALU.add)

        y_banks, y_tiles = [], []
        for t in range(PACK):
            w_plane = keep.tile([P, 2 * P], U8, name="w_plane%d" % t, tag="w_plane", bufs=2, align_bytes=MX_ALIGN)
            nc.vector.tensor_copy(w_plane[:], w_rows[:].rearrange("p (m t) -> p m t", t=PACK)[:, :, t])
            bank = psum.tile([P, S], F32, name="y_bank%d" % t)
            for i, codes in enumerate((w1_dealt[:, t, :], w2_dealt[t])):
                nc.tensor.matmul_mx(
                    out=bank[:],
                    lhsT=codes.bitcast(FP8X4),
                    lhsT_scale=w_plane[:, i * P:(i + 1) * P],
                    rhs=pair_words[:, i * S:(i + 1) * S].bitcast(FP8X4),
                    rhs_scale=pair_plane[:, i * S:(i + 1) * S],
                    start=(i == 0),
                    stop=(i == 1),
                )
            y = keep.tile([P, S], F32, name="y%d" % t)
            nc.vector.tensor_copy(y[:], bank[:])
            y_banks.append(bank)
            y_tiles.append(y)

        cand_bytes = keep.tile([P, C], U8, name="cand_bytes", tag="pair_plane_then_cand_bytes", align_bytes=MX_ALIGN)
        nc.vector.tensor_copy(cand_bytes[:], x_rows[:].indirect(cand_list[:]))
        cand_plane = scale_plane(cand_bytes, "cand_plane", "cand_plane")
        cand_words = keep.tile([P, C], U32, name="cand_words", tag="picked_words", align_bytes=MX_ALIGN)
        nc.vector.tensor_copy(cand_words[:], x_table[:].indirect(cand_list[:]))

        z_halves = [keep.tile([P, HALF, PACK], BF16, name="z%d" % h, align_bytes=MX_ALIGN) for h in range(2)]
        ds_tiles = [keep.tile([P, WINDOW], F32, name="ds%d" % t) for t in range(PACK)]
        sg_tiles = []

        def place_y(t):
            nc.scalar.activation(ds_tiles[t][:].indirect(n1_list[:]), y_tiles[t][:], ACT.Copy)

        def gate(t, first, last):
            if first == 0:
                if t < 2:
                    sg_tiles.append(keep.tile([P, S], F32, name="sg%d" % t, tag="w_plane", bufs=2, align_bytes=MX_ALIGN))
                else:
                    sg_tiles.append(keep.tile([P, S], F32, name="sg%d" % t))
            sg = sg_tiles[t]
            nc.scalar.activation(
                sg[:, first * HALF:last * HALF],
                ds_tiles[t][:].indirect(n2_list[:, first * HALF // GROUP:last * HALF // GROUP]),
                ACT.Sigmoid, bias=bias[:, t:t + 1], scale=slope[:, t:t + 1],
            )
            for h in range(first, last):
                cols = slice(h * HALF, (h + 1) * HALF)
                nc.vector.scalar_tensor_tensor(
                    z_halves[h][:, :, t], y_banks[t][:, cols], gain[:, t:t + 1], sg[:, cols], ALU.mult, ALU.mult
                )

        place_y(0)
        place_y(1)
        gate(0, 0, 2)
        place_y(2)
        gate(1, 0, 2)
        gate(2, 0, 1)
        place_y(3)
        gate(2, 1, 2)
        gate(3, 0, 1)
        gate(3, 1, 2)

        z_codes = keep.tile([P, S], U32, name="z_codes", align_bytes=MX_ALIGN)
        z_plane = keep.tile([P, S], U8, name="z_plane", align_bytes=MX_ALIGN)
        for h in range(2):
            cols = slice(h * HALF, (h + 1) * HALF)
            nc.vector.quantize_mx(
                out=z_codes[:, cols].bitcast(FP8X4), scales=z_plane[:, cols],
                in_=z_halves[h][:].rearrange("p j t -> p (j t)"),
            )

        s_tiles, others, pages = [], [], []

        def score(c):
            rows = slice(c * P, (c + 1) * P)
            s = keep.tile([P, WINDOW], F32, name="s%d" % c)
            pieces = 2 if c == 0 else 1
            width = S // pieces
            for piece in range(pieces):
                cols = slice(piece * width, (piece + 1) * width)
                bank = psum.tile([P, width], F32, name="s_bank%d_%d" % (c, piece),
                                 tag="y_bank0" if c == CAND_TILES - 1 else "s_bank%d_%d" % (c, piece))
                nc.tensor.matmul_mx(
                    out=bank[:],
                    lhsT=cand_words[:, rows].bitcast(FP8X4), lhsT_scale=cand_plane[:, rows],
                    rhs=z_codes[:, cols].bitcast(FP8X4), rhs_scale=z_plane[:, cols],
                    start=True, stop=True,
                )
                if c == 0:
                    nc.scalar.activation(s[:, cols], bank[:], ACT.Copy, scale=0.0625)
                else:
                    nc.vector.tensor_scalar(s[:, cols], bank[:], 0.0625, None, ALU.mult)
            s_tiles.append(s)

        def partner(c):
            other = keep.tile([P, S], F32, name="other%d" % c)
            nc.scalar.activation(other[:], s_tiles[c][:].indirect(n5_list[:]), ACT.Copy)
            others.append(other)

        def pick(c, op, name):
            picked = keep.tile([P, S], F32, name="%s%d" % (name, c))
            nc.vector.tensor_tensor(picked[:], s_tiles[c][:, :S], others[c][:], op)
            return picked

        def place_up(c, up):
            page = keep.tile([P, U], F32, name="page%d" % c)
            nc.scalar.activation(page[:].indirect(n3_list[:]), up[:], ACT.Copy)
            pages.append(page)

        def place_down(c, down):
            nc.scalar.activation(pages[c][:].indirect(n4_list[:]), down[:], ACT.Copy)
            nc.sync.dma_start(out[c * P:(c + 1) * P, :], pages[c][:])

        for c in range(CAND_TILES):
            score(c)
        for c in range(CAND_TILES):
            partner(c)
        for first in range(0, CAND_TILES, 2):
            pair = (first, first + 1)
            ups = [pick(c, ALU.max, "up") for c in pair]
            downs = [pick(c, ALU.min, "down") for c in pair]
            for c, up in zip(pair, ups):
                place_up(c, up)
            for c, down in zip(pair, downs):
                place_down(c, down)
